import numpy as np
import ml_dtypes


def mxq(x, axis, fmt="e4m3"):
    dtype, down = {"e4m3": (ml_dtypes.float8_e4m3fn, 7), "e5m2": (ml_dtypes.float8_e5m2, 14)}[fmt]
    v = np.moveaxis(np.asarray(x, np.float32).astype(ml_dtypes.bfloat16).astype(np.float64), axis, -1)
    blocks = v.reshape(v.shape[:-1] + (-1, 32))
    amax = np.abs(blocks).max(-1, keepdims=True)
    byte = np.maximum(np.where(amax > 0, np.frexp(amax)[1] - 1 + 127, 0) - down, 1)
    scale = np.exp2(byte - 127.0)
    codes = (blocks / scale).astype(np.float32).astype(dtype).astype(np.float64)
    return np.moveaxis((codes * scale).reshape(v.shape), -1, axis)


WIDE = False


def mx_kscale(k):
    if not WIDE:
        return np.ones(k)
    levels = np.array([10, -10, 5, -5, 0])
    if k % 512:
        return np.exp2(np.random.permutation(np.resize(levels, k // 32))).repeat(32)
    a = np.empty((k // 512, 16))
    for p in range(k // 512):
        a[p, :8] = np.random.permutation(np.resize(levels, 8))
        for g in range(8):
            far = levels[np.abs(levels - a[p, g]) >= 10]
            a[p, g + 8] = far[np.random.randint(len(far))]
    return np.exp2(a.ravel()).repeat(32)


def f64(x):
    return np.asarray(x).astype(np.float64)


def striped(idx):
    return np.tile(np.asarray(idx).reshape(-1, 16).T, (8, 1)).astype(np.uint16)


def unstriped(offs):
    return offs[:16].T.reshape(-1).astype(np.int64)


E2M1 = np.array([0.0, 0.5, 1.0, 1.5, 2.0, 3.0, 4.0, 6.0, -0.0, -0.5, -1.0, -1.5, -2.0, -3.0, -4.0, -6.0])


def pack_weight(w, fmt):
    k, n = w.shape
    w = f64(np.asarray(w, np.float32).astype(ml_dtypes.bfloat16)).reshape(k // 32, 32, n)
    amax = np.abs(w).max(1)
    if fmt == "e4m3":
        byte = np.frexp(amax)[1] - 1 + 127 - 7
    else:
        mant, ex = np.frexp(amax / 6.0)
        byte = np.where(mant > 0.5, ex, ex - 1) + 127
    byte = np.clip(np.where(amax > 0, byte, 1), 1, 254)
    scaled = (w * np.exp2(127.0 - byte)[:, None, :]).reshape(k, n).astype(np.float32)
    by_word = np.ascontiguousarray(scaled.reshape(k // 512, 128, 4, n).transpose(0, 1, 3, 2))
    if fmt == "e4m3":
        words = by_word.astype(ml_dtypes.float8_e4m3fn).view(np.uint8)
    else:
        c = by_word.astype(ml_dtypes.float4_e2m1fn).view(np.uint8) & 0xF
        words = (c[..., 0::2] | (c[..., 1::2] << 4)).reshape(k // 512, 128, 2 * n)
    return np.ascontiguousarray(words), np.ascontiguousarray(byte.astype(np.uint8).reshape(k // 512, 16, n))


def unpack_weight(words, scales, fmt):
    g, _, n = scales.shape
    words = np.ascontiguousarray(words).reshape(g, 128, n, -1)
    if fmt == "e4m3":
        vals = words.view(ml_dtypes.float8_e4m3fn).astype(np.float64)
    else:
        nib = np.empty((g, 128, n, 4), np.uint8)
        nib[..., 0::2] = words & 0xF
        nib[..., 1::2] = words >> 4
        vals = E2M1[nib]
    vals = vals * np.repeat(np.exp2(scales.astype(np.float64) - 127.0), 8, axis=1)[..., None]
    return vals.transpose(0, 1, 3, 2).reshape(g * 512, n)


def sigmoid(v):
    return 1.0 / (1.0 + np.exp(-v))


def bf(x):
    return np.asarray(x, np.float32).astype(ml_dtypes.bfloat16)


def planes(Y):
    r, m = Y.shape
    b = f64(bf(Y)).reshape(r // 32, 32, m)
    amax = np.abs(b).max(1)
    byte = np.clip(np.where(amax > 0, np.frexp(amax)[1] - 1 + 127 - 7, 1), 1, 254)
    codes = (b * np.exp2(127.0 - byte)[:, None, :]).reshape(r, m).astype(np.float32).astype(ml_dtypes.float8_e4m3fn).view(np.uint8)
    words = codes.reshape(r // 512, 128, 4, m).transpose(0, 1, 3, 2)
    return np.ascontiguousarray(words), np.ascontiguousarray(byte.astype(np.uint8).reshape(r // 512, 16, m))


D, T, I, Q, G, E = 512, 2048, 512, 512, 128, 512


def setup_inputs():
    n = np.random.standard_normal
    idx = np.random.permutation(T)[:I]
    fd = mx_kscale(D)
    fi = mx_kscale(I)
    ti = np.ones(T)
    ti[idx] = fi
    keysp = pack_weight(n((D, T)) / fd[:, None], "e2m1")
    return {
        "query": (n((D, Q)) * 1.0 / np.sqrt(D) * fd[:, None]).astype(np.float32),
        "keys_words": keysp[0],
        "keys_scales": keysp[1],
        "steep": (np.random.uniform(1.0, 3.0, (I, 1))).astype(np.float32),
        "bias": (np.random.uniform(-2.0, 0.0, (I, 1))).astype(np.float32),
        "us": (np.random.uniform(0.02, 0.1, (I, 1)) * fi[:, None]).astype(np.float32),
        "vals": (n((E, T)) / ti).astype(np.float32),
        "offs": striped(idx),
    }


def reference(query, keys_words, keys_scales, steep, bias, us, vals, offs):
    idx = unstriped(offs)
    keysu = unpack_weight(keys_words, keys_scales, "e2m1")
    keysidxg = keysu[:, idx]
    queryq = mxq(f64(query), 0, "e4m3")
    a = keysidxg.T @ queryq
    s = a.reshape(I, G, Q // G).max(axis=2)
    w = sigmoid(s * f64(steep) + f64(bias)) * f64(us)
    vt = f64(vals)[:, idx].T
    vtq = mxq(vt, 0, "e4m3")
    wq = mxq(w, 0, "e4m3")
    o = vtq.T @ wq
    words, scales = planes(o)
    return o, words, scales

@@ -1,0 +1,209 @@
+from contextlib import ExitStack
+
+import concourse.mybir as mybir
+from concourse.masks import make_identity
+
+D, T, I, Q, G, E = 512, 2048, 512, 512, 128, 512
+FLOPS = 2 * D * I * Q + 2 * I * E * G
+
+F32 = mybir.dt.float32
+BF16 = mybir.dt.bfloat16
+I32 = mybir.dt.int32
+U32 = mybir.dt.uint32
+U16 = mybir.dt.uint16
+U8 = mybir.dt.uint8
+FP8X4 = mybir.dt.float8_e4m3fn_x4
+FP4X4 = mybir.dt.float4_e2m1fn_x4
+ACT = mybir.ActivationFunctionType
+ALU = mybir.AluOpType
+
+P = 128
+PACK = 4
+HALF = G // 2
+
+
+def tile_attend_anyquestion_pl_kernel(tc, query, keys_words, keys_scales, steep, bias, us, vals, offs, out_0, out_1, out_2):
+    nc = tc.nc
+    with ExitStack() as ctx:
+        sb = ctx.enter_context(tc.tile_pool(name="sb", bufs=1))
+        ps = ctx.enter_context(tc.psum_pool(name="ps", bufs=1))
+
+        def tile(name, shape, dtype):
+            return sb.tile(shape, dtype, name=name, align_bytes=64)
+
+        key_scales = tile("key_scales", [P, T], U8)
+        nc.gpsimd.memset(key_scales[:].bitcast(I32), 0)
+        identity = tile("identity", [P, P], F32)
+        make_identity(nc, identity[:])
+
+        key_words = tile("key_words", [P, T], U16)
+        nc.sync.dma_start(key_words[:].bitcast(I32), keys_words[0].bitcast(I32))
+        offsets = tile("offsets", [P, I // 16], U16)
+        nc.sync.dma_start(offsets[:], offs)
+        for quad in range(4):
+            nc.sync.dma_start(
+                key_scales[32 * quad : 32 * quad + 4, :].bitcast(I32),
+                keys_scales[0, 4 * quad : 4 * quad + 4, :].bitcast(I32),
+            )
+
+        query_rows = query.rearrange("(p j) q -> p j q", j=PACK)
+        query_raw = []
+        for h in range(2):
+            raw = tile("query_raw%d" % h, [P, PACK, Q // 2], F32)
+            nc.sync.dma_start(raw[:], query_rows[:, :, h * (Q // 2) : (h + 1) * (Q // 2)])
+            query_raw.append(raw)
+
+        slot_vectors = []
+        for name, vector in (("steep", steep), ("bias", bias), ("us", us)):
+            columns = tile(name, [P, PACK], F32)
+            nc.sync.dma_start(columns[:], vector.rearrange("(p t) o -> p (t o)", t=PACK))
+            slot_vectors.append(columns)
+        steep_sb, bias_sb, us_sb = slot_vectors
+
+        vals_rows = vals.rearrange("(m r) t -> r m t", r=PACK)
+        vals_raw = []
+        for r in range(PACK):
+            raw = tile("vals_raw%d" % r, [P, T], F32)
+            nc.sync.dma_start(raw[:], vals_rows[r])
+            vals_raw.append(raw)
+
+        warm = tile("warm", [P, 1], F32)
+        warm_out = tile("warm_out", [P, 1], F32)
+        nc.vector.memset(warm[:], 0.0)
+        nc.scalar.activation(warm_out[:], warm[:], ACT.Sigmoid)
+
+        listed_words = tile("listed_words", [P, I], U16)
+        nc.vector.tensor_copy(listed_words[:], key_words[:].indirect(offsets[:]))
+        listed_scales = tile("listed_scales", [P, I], U8)
+        nc.vector.tensor_copy(listed_scales[:], key_scales[:].indirect(offsets[:]))
+
+        query_bf = tile("query_bf", [P, PACK, G, PACK], BF16)
+        for h in range(2):
+            dealt = query_bf[:, :, h * HALF : (h + 1) * HALF, :].rearrange("p r g j -> p g j r")
+            source = query_raw[h][:].rearrange("p j (g r) -> p g j r", r=PACK)
+            if h == 0:
+                nc.scalar.copy(dealt, source)
+            else:
+                nc.vector.tensor_copy(dealt, source)
+        query_codes = tile("query_codes", [P, PACK, G], U32)
+        query_scales = tile("query_scales", [P, PACK, G], U8)
+        scores = []
+        for r in range(PACK):
+            nc.vector.quantize_mx(
+                query_codes[:, r, :].bitcast(FP8X4),
+                query_scales[:, r, :],
+                query_bf[:, r, :, :].rearrange("p g j -> p (g j)"),
+            )
+            bank = ps.tile([P, I], F32, name="scores%d" % r)
+            nc.tensor.matmul_mx(
+                bank[:],
+                lhsT=query_codes[:, r, :].bitcast(FP8X4),
+                lhsT_scale=query_scales[:, r, :],
+                rhs=listed_words[:].bitcast(FP4X4),
+                rhs_scale=listed_scales[:],
+                start=True,
+                stop=True,
+            )
+            scores.append(bank)
+
+        def gather_and_turn(r, listed, turned_bf):
+            nc.vector.tensor_copy(listed[:], vals_raw[r][:].indirect(offsets[:]))
+            pairs = listed[:].bitcast(F32)
+            pairs_turned = ps.tile([P, 2, P], F32, name="pairs_turned%d" % (r % 2))
+            for u in range(2):
+                nc.tensor.transpose(pairs_turned[:, u, :], pairs[:, u : I // 2 : 2], identity[:])
+            nc.scalar.copy(turned_bf.bitcast(F32), pairs_turned[:].rearrange("p u m -> p m u"))
+
+        early_bf = tile("early_bf", [P, 2 * P, PACK], BF16)
+        gather_and_turn(0, tile("listed_vals0", [P, I], BF16), early_bf[:, :P, :])
+
+        best = tile("best0", [P, PACK, P], F32)
+        nc.scalar.copy(best[:], scores[0][:].rearrange("g (s t) -> g t s", t=PACK))
+        for r in range(1, PACK):
+            better = tile("vals_raw0" if r == 1 else "best%d" % r, [P, PACK, P], F32)
+            nc.vector.tensor_tensor(
+                better[:], scores[r][:].rearrange("g (s t) -> g t s", t=PACK), best[:], ALU.max
+            )
+            best = better
+
+        turned = ps.tile([P, PACK, G], F32, name="scores0")
+        for t in range(PACK):
+            nc.tensor.transpose(turned[:, t, :], best[:, t, :], identity[:])
+        gate = tile("gate", [P, PACK, G], F32)
+        weight = tile("weight", [P, PACK, G], F32)
+        for t in range(PACK):
+            nc.scalar.activation(
+                gate[:, t, :], turned[:, t, :], ACT.Sigmoid, bias=bias_sb[:, t : t + 1], scale=steep_sb[:, t : t + 1]
+            )
+        for t in range(PACK):
+            nc.scalar.activation(weight[:, t, :], gate[:, t, :], ACT.Copy, scale=us_sb[:, t : t + 1])
+        weight_bf = tile("weight_bf", [P, G, PACK], BF16)
+        nc.scalar.copy(weight_bf[:], weight[:].rearrange("p t g -> p g t"))
+
+        sums = [ps.tile([P, PACK, HALF], F32, name="sums%d" % h) for h in range(2)]
+        result = tile("result", [P, PACK, G], F32)
+        out_rows = out_0.rearrange("(m r) g -> m r g", r=PACK)
+
+        def multiply(r, codes, scales):
+            for h in range(2):
+                readers = slice(h * HALF, (h + 1) * HALF)
+                nc.tensor.matmul_mx(
+                    sums[h][:, r, :],
+                    lhsT=codes.bitcast(FP8X4),
+                    lhsT_scale=scales,
+                    rhs=weight_codes[:, readers].bitcast(FP8X4),
+                    rhs_scale=weight_scales[:, readers],
+                    start=True,
+                    stop=True,
+                )
+
+        def quantise(codes, scales, values):
+            nc.vector.quantize_mx(codes.bitcast(FP8X4), scales, values.rearrange("p m t -> p (m t)"))
+
+        gather_and_turn(1, tile("listed_vals1", [P, I], BF16), early_bf[:, P:, :])
+        third_bf = tile("third_bf", [P, P, PACK], BF16)
+        gather_and_turn(2, tile("listed_vals2", [P, I], BF16), third_bf[:])
+
+        early_codes = tile("vals_raw2", [P, 2 * P], U32)
+        early_scales = tile("early_scales", [P, 2 * P], U8)
+        quantise(early_codes[:], early_scales[:], early_bf[:])
+        weight_codes = tile("early_bf", [P, G], U32)
+        weight_scales = tile("weight_scales", [P, G], U8)
+        quantise(weight_codes[:], weight_scales[:], weight_bf[:])
+        for r in range(2):
+            multiply(r, early_codes[:, r * P : (r + 1) * P], early_scales[:, r * P : (r + 1) * P])
+
+        last_bf = tile("last_bf", [P, P, PACK], BF16)
+        gather_and_turn(3, tile("weight_bf", [P, I], BF16), last_bf[:])
+        third_codes = tile("vals_raw3", [P, P], U32)
+        third_scales = tile("third_scales", [P, P], U8)
+        quantise(third_codes[:], third_scales[:], third_bf[:])
+        multiply(2, third_codes[:], third_scales[:])
+        for h in range(2):
+            nc.scalar.copy(result[:, : PACK - 1, h * HALF : (h + 1) * HALF], sums[h][:, : PACK - 1, :])
+        nc.sync.dma_start(out_rows[:, : PACK - 1, :], result[:, : PACK - 1, :])
+        last_codes = tile("last_codes", [P, P], U32)
+        last_scales = tile("last_scales", [P, P], U8)
+        quantise(last_codes[:], last_scales[:], last_bf[:])
+        multiply(3, last_codes[:], last_scales[:])
+
+        result_bf = tile("result_bf", [P, G, PACK], BF16)
+        nc.vector.tensor_copy(result_bf[:, :HALF, :], sums[0][:].rearrange("p r g -> p g r"))
+        nc.scalar.copy(result_bf[:, HALF:, :], sums[1][:].rearrange("p r g -> p g r"))
+        result_codes = tile("result_codes", [P, G], U32)
+        result_scales = tile("result_scales", [P, G], U8)
+        nc.vector.quantize_mx(
+            result_codes[:].bitcast(FP8X4), result_scales[:], result_bf[:].rearrange("p g r -> p (g r)")
+        )
+        for h in (1, 0):
+            nc.scalar.copy(result[:, PACK - 1, h * HALF : (h + 1) * HALF], sums[h][:, PACK - 1, :])
+        nc.scalar.dma_start(out_rows[:, PACK - 1, :], result[:, PACK - 1, :])
+        nc.sync.dma_start(
+            out_1[0].rearrange("p g r -> p (g r)").bitcast(I32), result_codes[:].bitcast(I32)
+        )
+        for quad in range(4):
+            queue = nc.sync if quad % 2 == 0 else nc.scalar
+            queue.dma_start(
+                out_2[0, 4 * quad : 4 * quad + 4, :].bitcast(I32),
+                result_scales[32 * quad : 32 * quad + 4, :].bitcast(I32),
+            )

@@ -46,13 +46,23 @@ def tile_attend_anyquestion_pl_kernel(tc, query, keys_words, keys_scales, steep,
                 keys_scales[0, 4 * quad : 4 * quad + 4, :].bitcast(I32),
             )
 
+        HQ = Q // 2
         query_rows = query.rearrange("(p j) q -> p j q", j=PACK)
         query_raw = []
         for h in range(2):
-            raw = tile("query_raw%d" % h, [P, PACK, Q // 2], F32)
-            nc.sync.dma_start(raw[:], query_rows[:, :, h * (Q // 2) : (h + 1) * (Q // 2)])
+            raw = tile("query_raw%d" % h, [P, PACK, HQ], F32)
+            nc.sync.dma_start(raw[:], query_rows[:, :, h * HQ : (h + 1) * HQ])
             query_raw.append(raw)
 
+        vals_rows = vals.rearrange("(m r) t -> r m t", r=PACK)
+        vals_raw = []
+
+        def load_vals(r):
+            raw = tile("vals_raw%d" % r, [P, T], F32)
+            nc.sync.dma_start(raw[:], vals_rows[r])
+            vals_raw.append(raw)
+
+        load_vals(0)
         slot_vectors = []
         for name, vector in (("steep", steep), ("bias", bias), ("us", us)):
             columns = tile(name, [P, PACK], F32)
@@ -60,12 +70,8 @@ def tile_attend_anyquestion_pl_kernel(tc, query, keys_words, keys_scales, steep,
             slot_vectors.append(columns)
         steep_sb, bias_sb, us_sb = slot_vectors
 
-        vals_rows = vals.rearrange("(m r) t -> r m t", r=PACK)
-        vals_raw = []
-        for r in range(PACK):
-            raw = tile("vals_raw%d" % r, [P, T], F32)
-            nc.sync.dma_start(raw[:], vals_rows[r])
-            vals_raw.append(raw)
+        for r in range(1, PACK):
+            load_vals(r)
 
         warm = tile("warm", [P, 1], F32)
         warm_out = tile("warm_out", [P, 1], F32)
@@ -77,34 +83,57 @@ def tile_attend_anyquestion_pl_kernel(tc, query, keys_words, keys_scales, steep,
         listed_scales = tile("listed_scales", [P, I], U8)
         nc.vector.tensor_copy(listed_scales[:], key_scales[:].indirect(offsets[:]))
 
-        query_bf = tile("query_bf", [P, PACK, G, PACK], BF16)
+        key_codes = tile("key_codes", [P, PACK, P], U16)
+        nc.vector.tensor_copy(key_codes[:], listed_words[:].rearrange("p (s t) -> p t s", t=PACK))
+        key_bytes = tile("key_bytes", [P, PACK, P], U8)
+        nc.vector.tensor_copy(key_bytes[:], listed_scales[:].rearrange("p (s t) -> p t s", t=PACK))
+
+        query_mx = []
         for h in range(2):
-            dealt = query_bf[:, :, h * HALF : (h + 1) * HALF, :].rearrange("p r g j -> p g j r")
-            source = query_raw[h][:].rearrange("p j (g r) -> p g j r", r=PACK)
-            if h == 0:
-                nc.scalar.copy(dealt, source)
-            else:
-                nc.vector.tensor_copy(dealt, source)
-        query_codes = tile("query_codes", [P, PACK, G], U32)
-        query_scales = tile("query_scales", [P, PACK, G], U8)
-        scores = []
-        for r in range(PACK):
-            nc.vector.quantize_mx(
-                query_codes[:, r, :].bitcast(FP8X4),
-                query_scales[:, r, :],
-                query_bf[:, r, :, :].rearrange("p g j -> p (g j)"),
+            rounded = tile("query_bf%d" % h, [P, HQ, PACK], BF16)
+            target = rounded[:].rearrange("p (c i) j -> p c j i", i=4)
+            source = query_raw[h][:].rearrange("p j (c i) -> p c j i", i=4)
+            nc.scalar.copy(target, source)
+            codes = tile("query_codes%d" % h, [P, HQ], U32)
+            scales = tile("query_scales%d" % h, [P, HQ], U8)
+            nc.vector.quantize_mx(codes[:].bitcast(FP8X4), scales[:], rounded[:].rearrange("p q j -> p (q j)"))
+            query_mx.append((codes, scales))
+
+        scores = [ps.tile([P, Q], F32, name="scores%d" % t) for t in range(PACK)]
+        best = tile("best", [P, PACK, G], F32)
+        for h in range(2):
+            codes, scales = query_mx[h]
+            for t in range(PACK):
+                part = scores[t][:, h * HQ : (h + 1) * HQ]
+                nc.tensor.matmul_mx(
+                    part,
+                    lhsT=key_codes[:, t, :].bitcast(FP4X4),
+                    lhsT_scale=key_bytes[:, t, :],
+                    rhs=codes[:].bitcast(FP8X4),
+                    rhs_scale=scales[:],
+                    start=True,
+                    stop=True,
+                )
+                nc.vector.tensor_reduce(
+                    best[:, t, h * HALF : (h + 1) * HALF],
+                    part.rearrange("p (g r) -> p g r", r=Q // G),
+                    mybir.AxisListType.X,
+                    ALU.max,
+                )
+
+        gate = tile("gate", [P, PACK, G], F32)
+        weight = tile("weight", [P, PACK, G], F32)
+        for t in range(PACK):
+            nc.scalar.activation(
+                gate[:, t, :], best[:, t, :], ACT.Sigmoid, bias=bias_sb[:, t : t + 1], scale=steep_sb[:, t : t + 1]
             )
-            bank = ps.tile([P, I], F32, name="scores%d" % r)
-            nc.tensor.matmul_mx(
-                bank[:],
-                lhsT=query_codes[:, r, :].bitcast(FP8X4),
-                lhsT_scale=query_scales[:, r, :],
-                rhs=listed_words[:].bitcast(FP4X4),
-                rhs_scale=listed_scales[:],
-                start=True,
-                stop=True,
-            )
-            scores.append(bank)
+            nc.scalar.activation(weight[:, t, :], gate[:, t, :], ACT.Copy, scale=us_sb[:, t : t + 1])
+        weight_bf = tile("weight_bf", [P, G, PACK], BF16)
+        nc.scalar.copy(weight_bf[:], weight[:].rearrange("p t g -> p g t"))
+
+        sums = [ps.tile([P, PACK, HALF], F32, name="sums%d" % h) for h in range(2)]
+        result = tile("result", [P, PACK, G], F32)
+        out_rows = out_0.rearrange("(m r) g -> m r g", r=PACK)
 
         def gather_and_turn(r, listed, turned_bf):
             nc.vector.tensor_copy(listed[:], vals_raw[r][:].indirect(offsets[:]))
@@ -113,36 +142,6 @@ def tile_attend_anyquestion_pl_kernel(tc, query, keys_words, keys_scales, steep,
             for u in range(2):
                 nc.tensor.transpose(pairs_turned[:, u, :], pairs[:, u : I // 2 : 2], identity[:])
             nc.scalar.copy(turned_bf.bitcast(F32), pairs_turned[:].rearrange("p u m -> p m u"))
-
-        early_bf = tile("early_bf", [P, 2 * P, PACK], BF16)
-        gather_and_turn(0, tile("listed_vals0", [P, I], BF16), early_bf[:, :P, :])
-
-        best = tile("best0", [P, PACK, P], F32)
-        nc.scalar.copy(best[:], scores[0][:].rearrange("g (s t) -> g t s", t=PACK))
-        for r in range(1, PACK):
-            better = tile("vals_raw0" if r == 1 else "best%d" % r, [P, PACK, P], F32)
-            nc.vector.tensor_tensor(
-                better[:], scores[r][:].rearrange("g (s t) -> g t s", t=PACK), best[:], ALU.max
-            )
-            best = better
-
-        turned = ps.tile([P, PACK, G], F32, name="scores0")
-        for t in range(PACK):
-            nc.tensor.transpose(turned[:, t, :], best[:, t, :], identity[:])
-        gate = tile("gate", [P, PACK, G], F32)
-        weight = tile("weight", [P, PACK, G], F32)
-        for t in range(PACK):
-            nc.scalar.activation(
-                gate[:, t, :], turned[:, t, :], ACT.Sigmoid, bias=bias_sb[:, t : t + 1], scale=steep_sb[:, t : t + 1]
-            )
-        for t in range(PACK):
-            nc.scalar.activation(weight[:, t, :], gate[:, t, :], ACT.Copy, scale=us_sb[:, t : t + 1])
-        weight_bf = tile("weight_bf", [P, G, PACK], BF16)
-        nc.scalar.copy(weight_bf[:], weight[:].rearrange("p t g -> p g t"))
-
-        sums = [ps.tile([P, PACK, HALF], F32, name="sums%d" % h) for h in range(2)]
-        result = tile("result", [P, PACK, G], F32)
-        out_rows = out_0.rearrange("(m r) g -> m r g", r=PACK)
 
         def multiply(r, codes, scales):
             for h in range(2):
@@ -160,28 +159,30 @@ def tile_attend_anyquestion_pl_kernel(tc, query, keys_words, keys_scales, steep,
         def quantise(codes, scales, values):
             nc.vector.quantize_mx(codes.bitcast(FP8X4), scales, values.rearrange("p m t -> p (m t)"))
 
-        gather_and_turn(1, tile("listed_vals1", [P, I], BF16), early_bf[:, P:, :])
+        early_bf = tile("early_bf", [P, 2 * P, PACK], BF16)
+        for r in range(2):
+            gather_and_turn(r, tile("listed_vals%d" % r, [P, I], BF16), early_bf[:, r * P : (r + 1) * P, :])
         third_bf = tile("third_bf", [P, P, PACK], BF16)
         gather_and_turn(2, tile("listed_vals2", [P, I], BF16), third_bf[:])
 
-        early_codes = tile("vals_raw2", [P, 2 * P], U32)
+        early_codes = tile("vals_raw2", [P, 2 * P + G], U32)
         early_scales = tile("early_scales", [P, 2 * P], U8)
-        quantise(early_codes[:], early_scales[:], early_bf[:])
-        weight_codes = tile("early_bf", [P, G], U32)
+        quantise(early_codes[:, : 2 * P], early_scales[:], early_bf[:])
+        weight_codes = early_codes[:, 2 * P :]
         weight_scales = tile("weight_scales", [P, G], U8)
-        quantise(weight_codes[:], weight_scales[:], weight_bf[:])
+        quantise(weight_codes, weight_scales[:], weight_bf[:])
         for r in range(2):
             multiply(r, early_codes[:, r * P : (r + 1) * P], early_scales[:, r * P : (r + 1) * P])
+        for h in range(2):
+            nc.scalar.copy(result[:, :2, h * HALF : (h + 1) * HALF], sums[h][:, :2, :])
+        nc.sync.dma_start(out_rows[:, :2, :], result[:, :2, :])
 
         last_bf = tile("last_bf", [P, P, PACK], BF16)
-        gather_and_turn(3, tile("weight_bf", [P, I], BF16), last_bf[:])
+        gather_and_turn(3, tile("listed_vals3", [P, I], BF16), last_bf[:])
         third_codes = tile("vals_raw3", [P, P], U32)
         third_scales = tile("third_scales", [P, P], U8)
         quantise(third_codes[:], third_scales[:], third_bf[:])
         multiply(2, third_codes[:], third_scales[:])
-        for h in range(2):
-            nc.scalar.copy(result[:, : PACK - 1, h * HALF : (h + 1) * HALF], sums[h][:, : PACK - 1, :])
-        nc.sync.dma_start(out_rows[:, : PACK - 1, :], result[:, : PACK - 1, :])
         last_codes = tile("last_codes", [P, P], U32)
         last_scales = tile("last_scales", [P, P], U8)
         quantise(last_codes[:], last_scales[:], last_bf[:])
@@ -196,8 +197,8 @@ def tile_attend_anyquestion_pl_kernel(tc, query, keys_words, keys_scales, steep,
             result_codes[:].bitcast(FP8X4), result_scales[:], result_bf[:].rearrange("p g r -> p (g r)")
         )
         for h in (1, 0):
-            nc.scalar.copy(result[:, PACK - 1, h * HALF : (h + 1) * HALF], sums[h][:, PACK - 1, :])
-        nc.scalar.dma_start(out_rows[:, PACK - 1, :], result[:, PACK - 1, :])
+            nc.scalar.copy(result[:, 2:, h * HALF : (h + 1) * HALF], sums[h][:, 2:, :])
+        nc.scalar.dma_start(out_rows[:, 2:, :], result[:, 2:, :])
         nc.sync.dma_start(
             out_1[0].rearrange("p g r -> p (g r)").bitcast(I32), result_codes[:].bitcast(I32)
         )

@@ -32,7 +32,8 @@ def tile_attend_anyquestion_pl_kernel(tc, query, keys_words, keys_scales, steep,
             return sb.tile(shape, dtype, name=name, align_bytes=64)
 
         key_scales = tile("key_scales", [P, T], U8)
-        nc.gpsimd.memset(key_scales[:].bitcast(I32), 0)
+        nc.vector.memset(key_scales[:, : T // 2].bitcast(I32), 0)
+        nc.gpsimd.memset(key_scales[:, T // 2 :].bitcast(I32), 0)
         identity = tile("identity", [P, P], F32)
         make_identity(nc, identity[:])
 
@@ -54,15 +55,6 @@ def tile_attend_anyquestion_pl_kernel(tc, query, keys_words, keys_scales, steep,
             nc.sync.dma_start(raw[:], query_rows[:, :, h * HQ : (h + 1) * HQ])
             query_raw.append(raw)
 
-        vals_rows = vals.rearrange("(m r) t -> r m t", r=PACK)
-        vals_raw = []
-
-        def load_vals(r):
-            raw = tile("vals_raw%d" % r, [P, T], F32)
-            nc.sync.dma_start(raw[:], vals_rows[r])
-            vals_raw.append(raw)
-
-        load_vals(0)
         slot_vectors = []
         for name, vector in (("steep", steep), ("bias", bias), ("us", us)):
             columns = tile(name, [P, PACK], F32)
@@ -70,8 +62,12 @@ def tile_attend_anyquestion_pl_kernel(tc, query, keys_words, keys_scales, steep,
             slot_vectors.append(columns)
         steep_sb, bias_sb, us_sb = slot_vectors
 
-        for r in range(1, PACK):
-            load_vals(r)
+        vals_rows = vals.rearrange("(m r) t -> r m t", r=PACK)
+        vals_raw = []
+        for r in range(PACK):
+            raw = tile("vals_raw%d" % r, [P, T], F32)
+            nc.sync.dma_start(raw[:], vals_rows[r])
+            vals_raw.append(raw)
 
         warm = tile("warm", [P, 1], F32)
         warm_out = tile("warm_out", [P, 1], F32)
@@ -83,10 +79,14 @@ def tile_attend_anyquestion_pl_kernel(tc, query, keys_words, keys_scales, steep,
         listed_scales = tile("listed_scales", [P, I], U8)
         nc.vector.tensor_copy(listed_scales[:], key_scales[:].indirect(offsets[:]))
 
-        key_codes = tile("key_codes", [P, PACK, P], U16)
-        nc.vector.tensor_copy(key_codes[:], listed_words[:].rearrange("p (s t) -> p t s", t=PACK))
-        key_bytes = tile("key_bytes", [P, PACK, P], U8)
-        nc.vector.tensor_copy(key_bytes[:], listed_scales[:].rearrange("p (s t) -> p t s", t=PACK))
+        def deal(name, listed, dtype, pair):
+            dealt = tile("%s%d" % (name, pair), [P, 2, P], dtype)
+            by_place = listed[:].rearrange("p (s t) -> p t s", t=PACK)
+            nc.vector.tensor_copy(dealt[:], by_place[:, 2 * pair : 2 * pair + 2, :])
+            return dealt
+
+        key_codes = [deal("key_codes", listed_words, U16, 0)]
+        key_bytes = [deal("key_bytes", listed_scales, U8, 0)]
 
         query_mx = []
         for h in range(2):
@@ -98,17 +98,20 @@ def tile_attend_anyquestion_pl_kernel(tc, query, keys_words, keys_scales, steep,
             scales = tile("query_scales%d" % h, [P, HQ], U8)
             nc.vector.quantize_mx(codes[:].bitcast(FP8X4), scales[:], rounded[:].rearrange("p q j -> p (q j)"))
             query_mx.append((codes, scales))
+            if h == 0:
+                key_codes.append(deal("key_codes", listed_words, U16, 1))
+                key_bytes.append(deal("key_bytes", listed_scales, U8, 1))
 
         scores = [ps.tile([P, Q], F32, name="scores%d" % t) for t in range(PACK)]
-        best = tile("best", [P, PACK, G], F32)
+        best = tile("query_bf1", [P, PACK, G], F32)
         for h in range(2):
             codes, scales = query_mx[h]
             for t in range(PACK):
                 part = scores[t][:, h * HQ : (h + 1) * HQ]
                 nc.tensor.matmul_mx(
                     part,
-                    lhsT=key_codes[:, t, :].bitcast(FP4X4),
-                    lhsT_scale=key_bytes[:, t, :],
+                    lhsT=key_codes[t // 2][:, t % 2, :].bitcast(FP4X4),
+                    lhsT_scale=key_bytes[t // 2][:, t % 2, :],
                     rhs=codes[:].bitcast(FP8X4),
                     rhs_scale=scales[:],
                     start=True,

from contextlib import ExitStack

import concourse.mybir as mybir
from concourse.masks import make_identity

D, T, I, Q, G, E = 512, 2048, 512, 512, 128, 512
FLOPS = 2 * D * I * Q + 2 * I * E * G

F32 = mybir.dt.float32
BF16 = mybir.dt.bfloat16
I32 = mybir.dt.int32
U32 = mybir.dt.uint32
U16 = mybir.dt.uint16
U8 = mybir.dt.uint8
FP8X4 = mybir.dt.float8_e4m3fn_x4
FP4X4 = mybir.dt.float4_e2m1fn_x4
ACT = mybir.ActivationFunctionType
ALU = mybir.AluOpType

P = 128
PACK = 4
HALF = G // 2


def tile_attend_anyquestion_pl_kernel(tc, query, keys_words, keys_scales, steep, bias, us, vals, offs, out_0, out_1, out_2):
    nc = tc.nc
    with ExitStack() as ctx:
        sb = ctx.enter_context(tc.tile_pool(name="sb", bufs=1))
        ps = ctx.enter_context(tc.psum_pool(name="ps", bufs=1))

        def tile(name, shape, dtype):
            return sb.tile(shape, dtype, name=name, align_bytes=64)

        key_scales = tile("key_scales", [P, T], U8)
        nc.vector.memset(key_scales[:, : T // 2].bitcast(I32), 0)
        nc.gpsimd.memset(key_scales[:, T // 2 :].bitcast(I32), 0)
        identity = tile("identity", [P, P], F32)
        make_identity(nc, identity[:])

        key_words = tile("key_words", [P, T], U16)
        nc.sync.dma_start(key_words[:].bitcast(I32), keys_words[0].bitcast(I32))
        offsets = tile("offsets", [P, I // 16], U16)
        nc.sync.dma_start(offsets[:], offs)
        for quad in range(4):
            nc.sync.dma_start(
                key_scales[32 * quad : 32 * quad + 4, :].bitcast(I32),
                keys_scales[0, 4 * quad : 4 * quad + 4, :].bitcast(I32),
            )

        HQ = Q // 2
        query_rows = query.rearrange("(p j) q -> p j q", j=PACK)
        query_raw = []
        for h in range(2):
            raw = tile("query_raw%d" % h, [P, PACK, HQ], F32)
            nc.sync.dma_start(raw[:], query_rows[:, :, h * HQ : (h + 1) * HQ])
            query_raw.append(raw)

        slot_vectors = []
        for name, vector in (("steep", steep), ("bias", bias), ("us", us)):
            columns = tile(name, [P, PACK], F32)
            nc.sync.dma_start(columns[:], vector.rearrange("(p t) o -> p (t o)", t=PACK))
            slot_vectors.append(columns)
        steep_sb, bias_sb, us_sb = slot_vectors

        vals_rows = vals.rearrange("(m r) t -> r m t", r=PACK)
        vals_raw = []
        for r in range(PACK):
            raw = tile("vals_raw%d" % r, [P, T], F32)
            nc.sync.dma_start(raw[:], vals_rows[r])
            vals_raw.append(raw)

        warm = tile("warm", [P, 1], F32)
        warm_out = tile("warm_out", [P, 1], F32)
        nc.vector.memset(warm[:], 0.0)
        nc.scalar.activation(warm_out[:], warm[:], ACT.Sigmoid)

        listed_words = tile("listed_words", [P, I], U16)
        nc.vector.tensor_copy(listed_words[:], key_words[:].indirect(offsets[:]))
        listed_scales = tile("listed_scales", [P, I], U8)
        nc.vector.tensor_copy(listed_scales[:], key_scales[:].indirect(offsets[:]))

        def deal(name, listed, dtype, pair):
            dealt = tile("%s%d" % (name, pair), [P, 2, P], dtype)
            by_place = listed[:].rearrange("p (s t) -> p t s", t=PACK)
            nc.vector.tensor_copy(dealt[:], by_place[:, 2 * pair : 2 * pair + 2, :])
            return dealt

        key_codes = [deal("key_codes", listed_words, U16, 0)]
        key_bytes = [deal("key_bytes", listed_scales, U8, 0)]

        query_mx = []
        for h in range(2):
            rounded = tile("query_bf%d" % h, [P, HQ, PACK], BF16)
            target = rounded[:].rearrange("p (c i) j -> p c j i", i=4)
            source = query_raw[h][:].rearrange("p j (c i) -> p c j i", i=4)
            nc.scalar.copy(target, source)
            codes = tile("query_codes%d" % h, [P, HQ], U32)
            scales = tile("query_scales%d" % h, [P, HQ], U8)
            nc.vector.quantize_mx(codes[:].bitcast(FP8X4), scales[:], rounded[:].rearrange("p q j -> p (q j)"))
            query_mx.append((codes, scales))
            if h == 0:
                key_codes.append(deal("key_codes", listed_words, U16, 1))
                key_bytes.append(deal("key_bytes", listed_scales, U8, 1))

        scores = [ps.tile([P, Q], F32, name="scores%d" % t) for t in range(PACK)]
        best = tile("query_bf1", [P, PACK, G], F32)
        for h in range(2):
            codes, scales = query_mx[h]
            for t in range(PACK):
                part = scores[t][:, h * HQ : (h + 1) * HQ]
                nc.tensor.matmul_mx(
                    part,
                    lhsT=key_codes[t // 2][:, t % 2, :].bitcast(FP4X4),
                    lhsT_scale=key_bytes[t // 2][:, t % 2, :],
                    rhs=codes[:].bitcast(FP8X4),
                    rhs_scale=scales[:],
                    start=True,
                    stop=True,
                )
                nc.vector.tensor_reduce(
                    best[:, t, h * HALF : (h + 1) * HALF],
                    part.rearrange("p (g r) -> p g r", r=Q // G),
                    mybir.AxisListType.X,
                    ALU.max,
                )

        gate = tile("gate", [P, PACK, G], F32)
        weight = tile("weight", [P, PACK, G], F32)
        for t in range(PACK):
            nc.scalar.activation(
                gate[:, t, :], best[:, t, :], ACT.Sigmoid, bias=bias_sb[:, t : t + 1], scale=steep_sb[:, t : t + 1]
            )
            nc.scalar.activation(weight[:, t, :], gate[:, t, :], ACT.Copy, scale=us_sb[:, t : t + 1])
        weight_bf = tile("weight_bf", [P, G, PACK], BF16)
        nc.scalar.copy(weight_bf[:], weight[:].rearrange("p t g -> p g t"))

        sums = [ps.tile([P, PACK, HALF], F32, name="sums%d" % h) for h in range(2)]
        result = tile("result", [P, PACK, G], F32)
        out_rows = out_0.rearrange("(m r) g -> m r g", r=PACK)

        def gather_and_turn(r, listed, turned_bf):
            nc.vector.tensor_copy(listed[:], vals_raw[r][:].indirect(offsets[:]))
            pairs = listed[:].bitcast(F32)
            pairs_turned = ps.tile([P, 2, P], F32, name="pairs_turned%d" % (r % 2))
            for u in range(2):
                nc.tensor.transpose(pairs_turned[:, u, :], pairs[:, u : I // 2 : 2], identity[:])
            nc.scalar.copy(turned_bf.bitcast(F32), pairs_turned[:].rearrange("p u m -> p m u"))

        def multiply(r, codes, scales):
            for h in range(2):
                readers = slice(h * HALF, (h + 1) * HALF)
                nc.tensor.matmul_mx(
                    sums[h][:, r, :],
                    lhsT=codes.bitcast(FP8X4),
                    lhsT_scale=scales,
                    rhs=weight_codes[:, readers].bitcast(FP8X4),
                    rhs_scale=weight_scales[:, readers],
                    start=True,
                    stop=True,
                )

        def quantise(codes, scales, values):
            nc.vector.quantize_mx(codes.bitcast(FP8X4), scales, values.rearrange("p m t -> p (m t)"))

        early_bf = tile("early_bf", [P, 2 * P, PACK], BF16)
        for r in range(2):
            gather_and_turn(r, tile("listed_vals%d" % r, [P, I], BF16), early_bf[:, r * P : (r + 1) * P, :])
        third_bf = tile("third_bf", [P, P, PACK], BF16)
        gather_and_turn(2, tile("listed_vals2", [P, I], BF16), third_bf[:])

        early_codes = tile("vals_raw2", [P, 2 * P + G], U32)
        early_scales = tile("early_scales", [P, 2 * P], U8)
        quantise(early_codes[:, : 2 * P], early_scales[:], early_bf[:])
        weight_codes = early_codes[:, 2 * P :]
        weight_scales = tile("weight_scales", [P, G], U8)
        quantise(weight_codes, weight_scales[:], weight_bf[:])
        for r in range(2):
            multiply(r, early_codes[:, r * P : (r + 1) * P], early_scales[:, r * P : (r + 1) * P])
        for h in range(2):
            nc.scalar.copy(result[:, :2, h * HALF : (h + 1) * HALF], sums[h][:, :2, :])
        nc.sync.dma_start(out_rows[:, :2, :], result[:, :2, :])

        last_bf = tile("last_bf", [P, P, PACK], BF16)
        gather_and_turn(3, tile("listed_vals3", [P, I], BF16), last_bf[:])
        third_codes = tile("vals_raw3", [P, P], U32)
        third_scales = tile("third_scales", [P, P], U8)
        quantise(third_codes[:], third_scales[:], third_bf[:])
        multiply(2, third_codes[:], third_scales[:])
        last_codes = tile("last_codes", [P, P], U32)
        last_scales = tile("last_scales", [P, P], U8)
        quantise(last_codes[:], last_scales[:], last_bf[:])
        multiply(3, last_codes[:], last_scales[:])

        result_bf = tile("result_bf", [P, G, PACK], BF16)
        nc.vector.tensor_copy(result_bf[:, :HALF, :], sums[0][:].rearrange("p r g -> p g r"))
        nc.scalar.copy(result_bf[:, HALF:, :], sums[1][:].rearrange("p r g -> p g r"))
        result_codes = tile("result_codes", [P, G], U32)
        result_scales = tile("result_scales", [P, G], U8)
        nc.vector.quantize_mx(
            result_codes[:].bitcast(FP8X4), result_scales[:], result_bf[:].rearrange("p g r -> p (g r)")
        )
        for h in (1, 0):
            nc.scalar.copy(result[:, 2:, h * HALF : (h + 1) * HALF], sums[h][:, 2:, :])
        nc.scalar.dma_start(out_rows[:, 2:, :], result[:, 2:, :])
        nc.sync.dma_start(
            out_1[0].rearrange("p g r -> p (g r)").bitcast(I32), result_codes[:].bitcast(I32)
        )
        for quad in range(4):
            queue = nc.sync if quad % 2 == 0 else nc.scalar
            queue.dma_start(
                out_2[0, 4 * quad : 4 * quad + 4, :].bitcast(I32),
                result_scales[32 * quad : 32 * quad + 4, :].bitcast(I32),
            )
